import numpy as np, ml_dtypes
CORES = [78,86,94,102,110,118]
N = 6
TK = 512
def setup_inputs(rng):
    return {"x": rng.standard_normal((N, 128, TK), dtype=np.float32).astype(ml_dtypes.bfloat16), "w": rng.standard_normal((N, 128, 128), dtype=np.float32).astype(ml_dtypes.bfloat16)}
def setup_inputs_big(rng):
    d = setup_inputs(rng)
    for k in ("x", "w"): d[k] = (d[k].astype(np.float32) * 1024.0).astype(d[k].dtype)
    return d
def setup_inputs_small(rng):
    d = setup_inputs(rng)
    for k in ("x", "w"): d[k] = (d[k].astype(np.float32) * (1 / 1024.0)).astype(d[k].dtype)
    return d
def setup_inputs_apart(rng):
    d = setup_inputs(rng)
    f = (10.0 ** rng.permutation(np.linspace(-1.5, 1.5, N))).astype(np.float32).reshape(N, 1, 1)
    for k in ("x", "w"): d[k] = (d[k].astype(np.float32) * f).astype(d[k].dtype)
    return d
def setup_inputs_neg(rng):
    d = setup_inputs(rng)
    d["x"] = (np.abs(d["x"].astype(np.float32)) * 1048576.0).astype(d["x"].dtype); d["w"] = (-np.abs(d["w"].astype(np.float32))).astype(d["w"].dtype)
    return d
def reference(x, w):
    X, W = x.astype(np.float64), w.astype(np.float64)
    y = np.stack([np.max([W[j].T @ X[r] for j in range(N)], axis=0) for r in range(N)])
    return {"y": y.astype(ml_dtypes.bfloat16)}

@@ -1,0 +1,98 @@
+from concourse.bass import DstId, RemoteDMATransfer
+from concourse.mybir import AluOpType
+
+N = 6
+M = 128
+TK = 512
+H = TK // 2
+
+SCRATCH = {
+    "wall": ("sbuf", [128, N * M], "bfloat16"),
+    "xs": ("sbuf", [128, TK], "bfloat16"),
+    "acc0": ("sbuf", [128, TK], "bfloat16"),
+    "acc1": ("sbuf", [128, TK], "bfloat16"),
+    "yb": ("sbuf", [128, TK], "bfloat16"),
+}
+for _i in range(N + 1):
+    SCRATCH["ps%d" % _i] = ("psum", [128, TK], "float32")
+
+SEMAPHORES = (["wl", "xl", "sent", "st0", "st1"] + ["arr%d" % s for s in range(N)]
+              + ["mm%d" % i for i in range(N + 1)] + ["v%d" % i for i in range(N + 1)])
+
+
+def _links(topo, a, b):
+    ca, cb = topo.chip(a), topo.chip(b)
+    if ca == cb:
+        return 0
+    return 1 if (topo.mates(ca, cb) or topo.same_plane(ca, cb)) else 2
+
+
+def _rounds(topo, cores):
+    n = len(cores)
+    return sorted(range(1, n), key=lambda k: (-sum(_links(topo, cores[s], cores[(s + k) % n]) for s in range(n)), k))
+
+
+def rank_program(g, core, T, topo):
+    r = T.rank_of(core)
+    if r is None:
+        return
+    cores = T.cores
+    rounds = _rounds(topo, cores)
+    slot = lambda j: T.wall[:, j * M:(j + 1) * M]
+
+    g.sync.dma_start(slot(r), T.w[:, :]).then_inc(T.sem.wl, 16)
+    g.sync.dma_start(T.xs[:, :], T.x[:, :]).then_inc(T.sem.xl, 16)
+
+    dsts = [cores[(r + k) % N] for k in rounds]
+    mask = topo.mask(core, dsts[0])
+    for d in dsts:
+        mask &= topo.mask(core, d)
+    neng = bin(mask).count("1")
+    ids = []
+    for d in dsts:
+        rid, pid, _se = topo.addr(d)
+        ids.append(DstId(rid=rid, pnc=pid))
+    g.wait_ge(T.sem.wl, 16)
+    g.remote_dma_fused(
+        [RemoteDMATransfer(dst_ids=ids, dma_engine_mask=mask, remote_sem=T.sem["arr%d" % r],
+                           src=slot(r), dsts=[slot(r) for _ in dsts])],
+        local_sem=T.sem.sent)
+
+    srcs = [(r - k) % N for k in rounds]
+    g.tensor.wait_ge(T.sem.wl, 16)
+    g.tensor.wait_ge(T.sem.xl, 16)
+    g.tensor.matmul(T.ps0[:, :], slot(r), T.xs[:, :], True, True).then_inc(T.sem.mm0, 1)
+    for i, s in enumerate(srcs[:-1], start=1):
+        g.tensor.wait_ge(T.sem["arr%d" % s], neng)
+        g.tensor.matmul(T["ps%d" % i][:, :], slot(s), T.xs[:, :], True, True).then_inc(T.sem["mm%d" % i], 1)
+    s = srcs[-1]
+    g.tensor.wait_ge(T.sem["arr%d" % s], neng)
+    for h in range(2):
+        i = N - 1 + h
+        g.tensor.matmul(T["ps%d" % i][:, 0:H], slot(s), T.xs[:, h * H:(h + 1) * H], True, True).then_inc(
+            T.sem["mm%d" % i], 1)
+
+    acc = [T.acc0, T.acc1]
+    g.vector.wait_ge(T.sem.mm0, 1)
+    g.vector.tensor_copy(acc[0][:, :], T.ps0[:, :]).then_inc(T.sem.v0, 1)
+    for i in range(1, N - 1):
+        g.vector.wait_ge(T.sem["mm%d" % i], 1)
+        g.vector.wait_ge(T.sem["v%d" % (i - 1)], 1)
+        g.vector.tensor_tensor(acc[i % 2][:, :], acc[(i - 1) % 2][:, :], T["ps%d" % i][:, :],
+                               AluOpType.max).then_inc(T.sem["v%d" % i], 1)
+    last = acc[(N - 2) % 2]
+    g.vector.wait_ge(T.sem["v%d" % (N - 2)], 1)
+    for h in range(2):
+        i = N - 1 + h
+        g.vector.wait_ge(T.sem["mm%d" % i], 1)
+        g.vector.tensor_tensor(T.yb[:, h * H:(h + 1) * H], last[:, h * H:(h + 1) * H], T["ps%d" % i][:, 0:H],
+                               AluOpType.max).then_inc(T.sem["v%d" % i], 1)
+
+    g.sync.wait_ge(T.sem["v%d" % (N - 1)], 1)
+    g.sync.dma_start(T.y[:, 0:H], T.yb[:, 0:H]).then_inc(T.sem.st0, 16)
+    g.scalar.wait_ge(T.sem["v%d" % N], 1)
+    g.scalar.dma_start(T.y[:, H:TK], T.yb[:, H:TK]).then_inc(T.sem.st1, 16)
+
+    g.wait_ge(T.sem.sent, neng)
+    g.sync.wait_ge(T.sem.st0, 16)
+    g.scalar.wait_ge(T.sem.st1, 16)

@@ -5,6 +5,9 @@ N = 6
 M = 128
 TK = 512
 H = TK // 2
+B = 4
+W = TK // B
+NBANK = 8
 
 SCRATCH = {
     "wall": ("sbuf", [128, N * M], "bfloat16"),
@@ -13,11 +16,11 @@ SCRATCH = {
     "acc1": ("sbuf", [128, TK], "bfloat16"),
     "yb": ("sbuf", [128, TK], "bfloat16"),
 }
-for _i in range(N + 1):
+for _i in range(NBANK):
     SCRATCH["ps%d" % _i] = ("psum", [128, TK], "float32")
 
 SEMAPHORES = (["wl", "xl", "sent", "st0", "st1"] + ["arr%d" % s for s in range(N)]
-              + ["mm%d" % i for i in range(N + 1)] + ["v%d" % i for i in range(N + 1)])
+              + ["mm%d" % i for i in range(N * B)] + ["v%d" % i for i in range(N * B)])
 
 
 def _links(topo, a, b):
@@ -29,7 +32,8 @@ def _links(topo, a, b):
 
 def _rounds(topo, cores):
     n = len(cores)
-    return sorted(range(1, n), key=lambda k: (-sum(_links(topo, cores[s], cores[(s + k) % n]) for s in range(n)), k))
+    rs = sorted(range(1, n), key=lambda k: (-sum(_links(topo, cores[s], cores[(s + k) % n]) for s in range(n)), k))
+    return [rs[-2]] + rs[:-2] + [rs[-1]]
 
 
 def rank_program(g, core, T, topo):
@@ -58,39 +62,40 @@ def rank_program(g, core, T, topo):
                            src=slot(r), dsts=[slot(r) for _ in dsts])],
         local_sem=T.sem.sent)
 
-    srcs = [(r - k) % N for k in rounds]
+    srcs = [r] + [(r - k) % N for k in rounds]
     g.tensor.wait_ge(T.sem.wl, 16)
     g.tensor.wait_ge(T.sem.xl, 16)
-    g.tensor.matmul(T.ps0[:, :], slot(r), T.xs[:, :], True, True).then_inc(T.sem.mm0, 1)
-    for i, s in enumerate(srcs[:-1], start=1):
-        g.tensor.wait_ge(T.sem["arr%d" % s], neng)
-        g.tensor.matmul(T["ps%d" % i][:, :], slot(s), T.xs[:, :], True, True).then_inc(T.sem["mm%d" % i], 1)
-    s = srcs[-1]
-    g.tensor.wait_ge(T.sem["arr%d" % s], neng)
-    for h in range(2):
-        i = N - 1 + h
-        g.tensor.matmul(T["ps%d" % i][:, 0:H], slot(s), T.xs[:, h * H:(h + 1) * H], True, True).then_inc(
-            T.sem["mm%d" % i], 1)
+    for i, s in enumerate(srcs):
+        if i > 0:
+            g.tensor.wait_ge(T.sem["arr%d" % s], neng)
+        for b in range(B):
+            q = i * B + b
+            if q >= NBANK:
+                g.tensor.wait_ge(T.sem["v%d" % (q - NBANK)], 1)
+            g.tensor.matmul(T["ps%d" % (q % NBANK)][:, 0:W], slot(s), T.xs[:, b * W:(b + 1) * W], True, True).then_inc(
+                T.sem["mm%d" % q], 1)
 
     acc = [T.acc0, T.acc1]
-    g.vector.wait_ge(T.sem.mm0, 1)
-    g.vector.tensor_copy(acc[0][:, :], T.ps0[:, :]).then_inc(T.sem.v0, 1)
-    for i in range(1, N - 1):
-        g.vector.wait_ge(T.sem["mm%d" % i], 1)
-        g.vector.wait_ge(T.sem["v%d" % (i - 1)], 1)
-        g.vector.tensor_tensor(acc[i % 2][:, :], acc[(i - 1) % 2][:, :], T["ps%d" % i][:, :],
-                               AluOpType.max).then_inc(T.sem["v%d" % i], 1)
-    last = acc[(N - 2) % 2]
-    g.vector.wait_ge(T.sem["v%d" % (N - 2)], 1)
-    for h in range(2):
-        i = N - 1 + h
-        g.vector.wait_ge(T.sem["mm%d" % i], 1)
-        g.vector.tensor_tensor(T.yb[:, h * H:(h + 1) * H], last[:, h * H:(h + 1) * H], T["ps%d" % i][:, 0:H],
-                               AluOpType.max).then_inc(T.sem["v%d" % i], 1)
+    for i in range(N):
+        for b in range(B):
+            q = i * B + b
+            cols = slice(b * W, (b + 1) * W)
+            ps = T["ps%d" % (q % NBANK)][:, 0:W]
+            g.vector.wait_ge(T.sem["mm%d" % q], 1)
+            if i == 0:
+                g.vector.tensor_copy(acc[0][:, cols], ps).then_inc(T.sem["v%d" % q], 1)
+                continue
+            g.vector.wait_ge(T.sem["v%d" % (q - B)], 1)
+            out = T.yb if i == N - 1 else acc[i % 2]
+            g.vector.tensor_tensor(out[:, cols], acc[(i - 1) % 2][:, cols], ps, AluOpType.max).then_inc(
+                T.sem["v%d" % q], 1)
 
-    g.sync.wait_ge(T.sem["v%d" % (N - 1)], 1)
+    q0 = (N - 1) * B
+    for b in range(B // 2):
+        g.sync.wait_ge(T.sem["v%d" % (q0 + b)], 1)
     g.sync.dma_start(T.y[:, 0:H], T.yb[:, 0:H]).then_inc(T.sem.st0, 16)
-    g.scalar.wait_ge(T.sem["v%d" % N], 1)
+    for b in range(B // 2, B):
+        g.scalar.wait_ge(T.sem["v%d" % (q0 + b)], 1)
     g.scalar.dma_start(T.y[:, H:TK], T.yb[:, H:TK]).then_inc(T.sem.st1, 16)
 
     g.wait_ge(T.sem.sent, neng)

from concourse.bass import DstId, RemoteDMATransfer
from concourse.mybir import AluOpType

N = 6
M = 128
TK = 512
H = TK // 2
B = 4
W = TK // B
NBANK = 8

SCRATCH = {
    "wall": ("sbuf", [128, N * M], "bfloat16"),
    "xs": ("sbuf", [128, TK], "bfloat16"),
    "acc0": ("sbuf", [128, TK], "bfloat16"),
    "acc1": ("sbuf", [128, TK], "bfloat16"),
    "yb": ("sbuf", [128, TK], "bfloat16"),
}
for _i in range(NBANK):
    SCRATCH["ps%d" % _i] = ("psum", [128, TK], "float32")

SEMAPHORES = (["wl", "xl", "sent", "st0", "st1"] + ["arr%d" % s for s in range(N)]
              + ["mm%d" % i for i in range(N * B)] + ["v%d" % i for i in range(N * B)])


def _links(topo, a, b):
    ca, cb = topo.chip(a), topo.chip(b)
    if ca == cb:
        return 0
    return 1 if (topo.mates(ca, cb) or topo.same_plane(ca, cb)) else 2


def _rounds(topo, cores):
    n = len(cores)
    rs = sorted(range(1, n), key=lambda k: (-sum(_links(topo, cores[s], cores[(s + k) % n]) for s in range(n)), k))
    return [rs[-2]] + rs[:-2] + [rs[-1]]


def rank_program(g, core, T, topo):
    r = T.rank_of(core)
    if r is None:
        return
    cores = T.cores
    rounds = _rounds(topo, cores)
    slot = lambda j: T.wall[:, j * M:(j + 1) * M]

    g.sync.dma_start(slot(r), T.w[:, :]).then_inc(T.sem.wl, 16)
    g.sync.dma_start(T.xs[:, :], T.x[:, :]).then_inc(T.sem.xl, 16)

    dsts = [cores[(r + k) % N] for k in rounds]
    mask = topo.mask(core, dsts[0])
    for d in dsts:
        mask &= topo.mask(core, d)
    neng = bin(mask).count("1")
    ids = []
    for d in dsts:
        rid, pid, _se = topo.addr(d)
        ids.append(DstId(rid=rid, pnc=pid))
    g.wait_ge(T.sem.wl, 16)
    g.remote_dma_fused(
        [RemoteDMATransfer(dst_ids=ids, dma_engine_mask=mask, remote_sem=T.sem["arr%d" % r],
                           src=slot(r), dsts=[slot(r) for _ in dsts])],
        local_sem=T.sem.sent)

    srcs = [r] + [(r - k) % N for k in rounds]
    g.tensor.wait_ge(T.sem.wl, 16)
    g.tensor.wait_ge(T.sem.xl, 16)
    for i, s in enumerate(srcs):
        if i > 0:
            g.tensor.wait_ge(T.sem["arr%d" % s], neng)
        for b in range(B):
            q = i * B + b
            if q >= NBANK:
                g.tensor.wait_ge(T.sem["v%d" % (q - NBANK)], 1)
            g.tensor.matmul(T["ps%d" % (q % NBANK)][:, 0:W], slot(s), T.xs[:, b * W:(b + 1) * W], True, True).then_inc(
                T.sem["mm%d" % q], 1)

    acc = [T.acc0, T.acc1]
    for i in range(N):
        for b in range(B):
            q = i * B + b
            cols = slice(b * W, (b + 1) * W)
            ps = T["ps%d" % (q % NBANK)][:, 0:W]
            g.vector.wait_ge(T.sem["mm%d" % q], 1)
            if i == 0:
                g.vector.tensor_copy(acc[0][:, cols], ps).then_inc(T.sem["v%d" % q], 1)
                continue
            g.vector.wait_ge(T.sem["v%d" % (q - B)], 1)
            out = T.yb if i == N - 1 else acc[i % 2]
            g.vector.tensor_tensor(out[:, cols], acc[(i - 1) % 2][:, cols], ps, AluOpType.max).then_inc(
                T.sem["v%d" % q], 1)

    q0 = (N - 1) * B
    for b in range(B // 2):
        g.sync.wait_ge(T.sem["v%d" % (q0 + b)], 1)
    g.sync.dma_start(T.y[:, 0:H], T.yb[:, 0:H]).then_inc(T.sem.st0, 16)
    for b in range(B // 2, B):
        g.scalar.wait_ge(T.sem["v%d" % (q0 + b)], 1)
    g.scalar.dma_start(T.y[:, H:TK], T.yb[:, H:TK]).then_inc(T.sem.st1, 16)

    g.wait_ge(T.sem.sent, neng)
    g.sync.wait_ge(T.sem.st0, 16)
    g.scalar.wait_ge(T.sem.st1, 16)
